import numpy as np
import ml_dtypes


def mxq(x, axis, fmt="e4m3"):
    dtype, down = {"e4m3": (ml_dtypes.float8_e4m3fn, 7), "e5m2": (ml_dtypes.float8_e5m2, 14)}[fmt]
    v = np.moveaxis(np.asarray(x, np.float32).astype(ml_dtypes.bfloat16).astype(np.float64), axis, -1)
    blocks = v.reshape(v.shape[:-1] + (-1, 32))
    amax = np.abs(blocks).max(-1, keepdims=True)
    byte = np.maximum(np.where(amax > 0, np.frexp(amax)[1] - 1 + 127, 0) - down, 1)
    scale = np.exp2(byte - 127.0)
    codes = (blocks / scale).astype(np.float32).astype(dtype).astype(np.float64)
    return np.moveaxis((codes * scale).reshape(v.shape), -1, axis)


WIDE = False


def mx_kscale(k):
    if not WIDE:
        return np.ones(k)
    levels = np.array([10, -10, 5, -5, 0])
    if k % 512:
        return np.exp2(np.random.permutation(np.resize(levels, k // 32))).repeat(32)
    a = np.empty((k // 512, 16))
    for p in range(k // 512):
        a[p, :8] = np.random.permutation(np.resize(levels, 8))
        for g in range(8):
            far = levels[np.abs(levels - a[p, g]) >= 10]
            a[p, g + 8] = far[np.random.randint(len(far))]
    return np.exp2(a.ravel()).repeat(32)


def f64(x):
    return np.asarray(x).astype(np.float64)


def striped(idx):
    return np.tile(np.asarray(idx).reshape(-1, 16).T, (8, 1)).astype(np.uint16)


def unstriped(offs):
    return offs[:16].T.reshape(-1).astype(np.int64)


E2M1 = np.array([0.0, 0.5, 1.0, 1.5, 2.0, 3.0, 4.0, 6.0, -0.0, -0.5, -1.0, -1.5, -2.0, -3.0, -4.0, -6.0])


def pack_weight(w, fmt):
    k, n = w.shape
    w = f64(np.asarray(w, np.float32).astype(ml_dtypes.bfloat16)).reshape(k // 32, 32, n)
    amax = np.abs(w).max(1)
    if fmt == "e4m3":
        byte = np.frexp(amax)[1] - 1 + 127 - 7
    else:
        mant, ex = np.frexp(amax / 6.0)
        byte = np.where(mant > 0.5, ex, ex - 1) + 127
    byte = np.clip(np.where(amax > 0, byte, 1), 1, 254)
    scaled = (w * np.exp2(127.0 - byte)[:, None, :]).reshape(k, n).astype(np.float32)
    by_word = np.ascontiguousarray(scaled.reshape(k // 512, 128, 4, n).transpose(0, 1, 3, 2))
    if fmt == "e4m3":
        words = by_word.astype(ml_dtypes.float8_e4m3fn).view(np.uint8)
    else:
        c = by_word.astype(ml_dtypes.float4_e2m1fn).view(np.uint8) & 0xF
        words = (c[..., 0::2] | (c[..., 1::2] << 4)).reshape(k // 512, 128, 2 * n)
    return np.ascontiguousarray(words), np.ascontiguousarray(byte.astype(np.uint8).reshape(k // 512, 16, n))


def unpack_weight(words, scales, fmt):
    g, _, n = scales.shape
    words = np.ascontiguousarray(words).reshape(g, 128, n, -1)
    if fmt == "e4m3":
        vals = words.view(ml_dtypes.float8_e4m3fn).astype(np.float64)
    else:
        nib = np.empty((g, 128, n, 4), np.uint8)
        nib[..., 0::2] = words & 0xF
        nib[..., 1::2] = words >> 4
        vals = E2M1[nib]
    vals = vals * np.repeat(np.exp2(scales.astype(np.float64) - 127.0), 8, axis=1)[..., None]
    return vals.transpose(0, 1, 3, 2).reshape(g * 512, n)


K, T, J, N = 1024, 2048, 512, 512


def setup_inputs():
    n = np.random.standard_normal
    idx = np.random.permutation(T)[:J]
    fk = mx_kscale(K)
    xqp = pack_weight(n((K, T)) / fk[:, None], "e4m3")
    wap = pack_weight(n((K, N)) * 1 / np.sqrt(K) * fk[:, None], "e2m1")
    return {
        "xq_words": xqp[0],
        "xq_scales": xqp[1],
        "wa_words": wap[0],
        "wa_scales": wap[1],
        "wb": (n((K, N)) * 1 / np.sqrt(K) * fk[:, None]).astype(np.float32),
        "ga": (np.random.uniform(0.4, 1.2, (1, J))).astype(np.float32),
        "offs": striped(idx),
    }


def reference(xq_words, xq_scales, wa_words, wa_scales, wb, ga, offs):
    idx = unstriped(offs)
    xqu = unpack_weight(xq_words, xq_scales, "e4m3")
    wau = unpack_weight(wa_words, wa_scales, "e2m1")
    xqidxg = xqu[:, idx]
    p = wau.T @ xqidxg
    wbq = mxq(f64(wb), 0, "e4m3")
    q = wbq.T @ xqidxg
    y = f64(ga) * (0.5 * (p + q) - 0.25 * np.abs(p - q))
    return y

@@ -1,0 +1,169 @@
+from contextlib import ExitStack
+
+import concourse.mybir as mybir
+
+K, T, J, N = 1024, 2048, 512, 512
+FLOPS = 2 * 2 * K * N * J
+
+F32 = mybir.dt.float32
+BF16 = mybir.dt.bfloat16
+I32 = mybir.dt.int32
+U32 = mybir.dt.uint32
+U16 = mybir.dt.uint16
+U8 = mybir.dt.uint8
+FP8X4 = mybir.dt.float8_e4m3fn_x4
+FP4X4 = mybir.dt.float4_e2m1fn_x4
+ALU = mybir.AluOpType
+ACT = mybir.ActivationFunctionType
+
+P = 128
+PACK = 4
+PASSES = K // (P * PACK)
+TILES = N // P
+QUADS = 4
+
+
+def tile_list_experts_disagreement_kernel(tc, xq_words, xq_scales, wa_words, wa_scales, wb, ga, offs, out):
+    nc = tc.nc
+    with ExitStack() as ctx:
+        keep = ctx.enter_context(tc.tile_pool(name="keep", bufs=1))
+        stage = ctx.enter_context(tc.tile_pool(name="stage", bufs=1))
+        psum = ctx.enter_context(tc.psum_pool(name="psum", bufs=1))
+
+        offsets = keep.tile([P, J // 16], U16, name="offsets")
+        nc.sync.dma_start(offsets[:], offs)
+
+        ga_rows = stage.tile([P, K * N // P], F32, name="ga_rows", offset=0)
+        nc.sync.dma_start(ga_rows[:, :PACK], ga.rearrange("o (p c) -> (o p) c", c=PACK))
+
+        xs_all = keep.tile([P, PASSES * T], U8, name="xs_all", align_bytes=64)
+        nc.vector.memset(xs_all[:].bitcast(I32), 0)
+        for qd in range(QUADS):
+            nc.scalar.dma_start(
+                xs_all[:].bitcast(I32)[32 * qd : 32 * qd + 4, :].rearrange("p (z c) -> p z c", z=PASSES),
+                xq_scales.bitcast(I32)[:, 4 * qd : 4 * qd + 4, :].rearrange("z r c -> r z c"),
+            )
+
+        blank = keep.tile([P, P], F32, name="blank", tag="xw_all1", align_bytes=64)
+        nc.vector.memset(blank[:], 0.0)
+        ident = keep.tile([P, P], F32, name="ident")
+        nc.gpsimd.affine_select(
+            out=ident[:],
+            in_=blank[:],
+            compare_op=ALU.not_equal,
+            fill=1.0,
+            base=0,
+            pattern=[[-1, P]],
+            channel_multiplier=1,
+        )
+        xw_all = [keep.tile([P, T], I32, name=f"xw_all{z}", tag=f"xw_all{z}", align_bytes=64) for z in range(PASSES)]
+        wa_w = keep.tile([P, PASSES * 2 * N], U8, name="wa_w", align_bytes=64)
+        nc.sync.dma_start(
+            wa_w[:].bitcast(I32).rearrange("p (z c) -> p z c", z=PASSES),
+            wa_words.bitcast(I32).rearrange("z p c -> p z c"),
+        )
+        nc.sync.dma_start(xw_all[0][:], xq_words[0].rearrange("p c r -> p (c r)").bitcast(I32))
+        nc.sync.dma_start(xw_all[1][:], xq_words[1].rearrange("p c r -> p (c r)").bitcast(I32))
+
+        wa_s = keep.tile([P, PASSES * N], U8, name="wa_s", align_bytes=64)
+        nc.vector.memset(wa_s[:].bitcast(I32), 0)
+        for qd in range(QUADS):
+            nc.scalar.dma_start(
+                wa_s[:].bitcast(I32)[32 * qd : 32 * qd + 4, :].rearrange("p (z c) -> p z c", z=PASSES),
+                wa_scales.bitcast(I32)[:, 4 * qd : 4 * qd + 4, :].rearrange("z r c -> r z c"),
+            )
+
+        ga_ps = psum.tile([P, PACK, P], F32, name="ga_ps")
+        for c in range(PACK):
+            nc.tensor.transpose(ga_ps[:, c, :], ga_rows[:, c : c + 1].to_broadcast([P, P]), ident[:])
+        ga_by_j = ga_ps[:].rearrange("p c n -> p n c")
+        ga4 = keep.tile([P, J], F32, name="ga4")
+        nc.scalar.activation(ga4[:].rearrange("p (n c) -> p n c", c=PACK), ga_by_j, ACT.Copy, scale=0.25)
+
+        xs = [keep.tile([P, J], U8, name=f"xs{z}", align_bytes=64) for z in range(PASSES)]
+        xw = [keep.tile([P, J], U32, name=f"xw{z}", align_bytes=64) for z in range(PASSES)]
+        for z in range(PASSES):
+            nc.vector.tensor_copy(xs[z][:], xs_all[:, z * T : (z + 1) * T].indirect(offsets[:]))
+        for z in range(PASSES):
+            nc.vector.tensor_copy(xw[z][:], xw_all[z][:].bitcast(U32).indirect(offsets[:]))
+
+        piece = PACK * P
+        raw = {}
+        for i in range(TILES):
+            for z in range(PASSES):
+                raw[i, z] = stage.tile([P, PACK, P], F32, name=f"raw{i}{z}", offset=(i * PASSES + z) * piece * 4)
+                nc.sync.dma_start(
+                    raw[i, z][:],
+                    wb[z * 512 : (z + 1) * 512, i * P : (i + 1) * P].rearrange("(p t) n -> p t n", t=PACK),
+                )
+
+        p_ps = [psum.tile([P, J], F32, name=f"p_ps{i}", tag=f"bank{i}") for i in range(TILES)]
+        for z in range(PASSES):
+            for i in range(TILES):
+                nc.tensor.matmul_mx(
+                    out=p_ps[i][:],
+                    lhsT=wa_w[:, z * 2 * N + i * 2 * P : z * 2 * N + (i + 1) * 2 * P].bitcast(FP4X4),
+                    lhsT_scale=wa_s[:, z * N + i * P : z * N + (i + 1) * P],
+                    rhs=xw[z][:].bitcast(FP8X4),
+                    rhs_scale=xs[z][:],
+                    start=(z == 0),
+                    stop=(z == PASSES - 1),
+                )
+
+        def second_expert(i):
+            q_ps = psum.tile([P, J], F32, name=f"q_ps{i}", tag=("bank0" if i == TILES - 1 else f"qbank{i}"))
+            for z in range(PASSES):
+                grouped = keep.tile([P, piece], BF16, name=f"grouped{i}{z}", tag=f"grouped{i}{z}", align_bytes=64)
+                nc.scalar.copy(
+                    grouped[:].rearrange("p (c i t) -> p c t i", i=4, t=PACK),
+                    raw[i, z][:].rearrange("p t (c i) -> p c t i", i=4),
+                )
+                wb_w = keep.tile([P, P], U32, name=f"wb_w{i}{z}", align_bytes=64)
+                wb_s = keep.tile([P, P], U8, name=f"wb_s{i}{z}", align_bytes=64)
+                nc.vector.quantize_mx(out=wb_w[:].bitcast(FP8X4), scales=wb_s[:], in_=grouped[:])
+                nc.tensor.matmul_mx(
+                    out=q_ps[:],
+                    lhsT=wb_w[:].bitcast(FP8X4),
+                    lhsT_scale=wb_s[:],
+                    rhs=xw[z][:].bitcast(FP8X4),
+                    rhs_scale=xs[z][:],
+                    start=(z == 0),
+                    stop=(z == PASSES - 1),
+                )
+            return q_ps
+
+        p_sb = keep.tile([P, J], F32, name="p_sb0")
+        nc.vector.tensor_copy(p_sb[:], p_ps[0][:])
+        q_ps = second_expert(0)
+        p_next = keep.tile([P, J], F32, name="p_sb1", tag="grouped01", align_bytes=64)
+        nc.vector.tensor_copy(p_next[:], p_ps[1][:])
+
+        for i in range(TILES):
+            low = keep.tile([P, J], F32, name=f"low{i}")
+            nc.vector.tensor_tensor(low[:], q_ps[:], p_sb[:], ALU.min)
+            if i + 1 < TILES:
+                q_next = second_expert(i + 1)
+            if 1 <= i < TILES - 1:
+                p_next = keep.tile([P, J], F32, name=f"p_sb{i + 1}", tag=f"grouped{i}1", align_bytes=64)
+                nc.scalar.copy(p_next[:], p_ps[i + 1][:])
+            part = keep.tile([P, J], F32, name=f"part{i}")
+            nc.vector.scalar_tensor_tensor(part[:], low[:], 2.0, q_ps[:], ALU.mult, ALU.add)
+            whole = keep.tile([P, J], F32, name=f"whole{i}")
+            if i < 2:
+                nc.gpsimd.tensor_tensor(whole[:], part[:], p_sb[:], ALU.add)
+            else:
+                nc.vector.tensor_tensor(whole[:], part[:], p_ps[i][:], ALU.add)
+            y = keep.tile([P, J], F32, name=f"y{i}")
+            if i < 3:
+                nc.gpsimd.tensor_tensor(y[:], whole[:], ga4[:], ALU.mult)
+            else:
+                nc.vector.scalar_tensor_tensor(
+                    y[:].rearrange("p (n c) -> p n c", c=PACK),
+                    whole[:].rearrange("p (n c) -> p n c", c=PACK),
+                    0.25,
+                    ga_by_j,
+                    ALU.mult,
+                    ALU.mult,
+                )
+            nc.sync.dma_start(out[i * P : (i + 1) * P, :], y[:])
+            p_sb, q_ps = p_next, q_next

@@ -18,60 +18,84 @@ ACT = mybir.ActivationFunctionType
 
 P = 128
 PACK = 4
-PASSES = K // (P * PACK)
+K_PASS = P * PACK
+PASSES = K // K_PASS
 TILES = N // P
 QUADS = 4
+KIB = 1024
+
+PIECES = [(i, z) for i in range(TILES) for z in range(PASSES)]
+AT_XW1 = 0
+AT_WAW = 8 * KIB
+AT_WAS = 10 * KIB
+AT_RAW = {piece: 11 * KIB + 2 * KIB * n for n, piece in enumerate(PIECES)}
+AT_GA = AT_RAW[1, 0]
+HELD_BYTES = 27 * KIB
+AT_LOW = [HELD_BYTES + 2 * KIB * i for i in range(TILES)]
 
 
 def tile_list_experts_disagreement_kernel(tc, xq_words, xq_scales, wa_words, wa_scales, wb, ga, offs, out):
     nc = tc.nc
     with ExitStack() as ctx:
         keep = ctx.enter_context(tc.tile_pool(name="keep", bufs=1))
-        stage = ctx.enter_context(tc.tile_pool(name="stage", bufs=1))
+        arena = ctx.enter_context(tc.tile_pool(name="arena", bufs=1))
         psum = ctx.enter_context(tc.psum_pool(name="psum", bufs=1))
+
+        def load_scale_rows(queue, plane, scales):
+            for qd in range(QUADS):
+                queue.dma_start(
+                    plane[:].bitcast(I32)[32 * qd : 32 * qd + 4, :].rearrange("p (z c) -> p z c", z=PASSES),
+                    scales.bitcast(I32)[:, 4 * qd : 4 * qd + 4, :].rearrange("z r c -> r z c"),
+                )
+
+        def load_wb(raw, z, n0, width):
+            rows = wb[z * K_PASS : (z + 1) * K_PASS, n0 : n0 + width]
+            nc.sync.dma_start(raw[:], rows.rearrange("(p t) n -> p t n", t=PACK))
 
         offsets = keep.tile([P, J // 16], U16, name="offsets")
         nc.sync.dma_start(offsets[:], offs)
-
-        ga_rows = stage.tile([P, K * N // P], F32, name="ga_rows", offset=0)
-        nc.sync.dma_start(ga_rows[:, :PACK], ga.rearrange("o (p c) -> (o p) c", c=PACK))
+        xw_all = [keep.tile([P, T], I32, name="xw_all0", align_bytes=64)]
+        nc.sync.dma_start(xw_all[0][:], xq_words[0].rearrange("p c r -> p (c r)").bitcast(I32))
 
         xs_all = keep.tile([P, PASSES * T], U8, name="xs_all", align_bytes=64)
         nc.vector.memset(xs_all[:].bitcast(I32), 0)
-        for qd in range(QUADS):
-            nc.scalar.dma_start(
-                xs_all[:].bitcast(I32)[32 * qd : 32 * qd + 4, :].rearrange("p (z c) -> p z c", z=PASSES),
-                xq_scales.bitcast(I32)[:, 4 * qd : 4 * qd + 4, :].rearrange("z r c -> r z c"),
-            )
+        load_scale_rows(nc.scalar, xs_all, xq_scales)
 
-        blank = keep.tile([P, P], F32, name="blank", tag="xw_all1", align_bytes=64)
-        nc.vector.memset(blank[:], 0.0)
+        blank = arena.tile([P, HELD_BYTES // 4], F32, name="blank", offset=0, align_bytes=64)
+        nc.vector.memset(blank[:, :P], 0.0)
         ident = keep.tile([P, P], F32, name="ident")
         nc.gpsimd.affine_select(
             out=ident[:],
-            in_=blank[:],
+            in_=blank[:, :P],
             compare_op=ALU.not_equal,
             fill=1.0,
             base=0,
             pattern=[[-1, P]],
             channel_multiplier=1,
         )
-        xw_all = [keep.tile([P, T], I32, name=f"xw_all{z}", tag=f"xw_all{z}", align_bytes=64) for z in range(PASSES)]
-        wa_w = keep.tile([P, PASSES * 2 * N], U8, name="wa_w", align_bytes=64)
+
+        ga_rows = arena.tile([P, (HELD_BYTES - AT_GA) // 4], F32, name="ga_rows", offset=AT_GA, align_bytes=64)
+        nc.sync.dma_start(ga_rows[:, :PACK], ga.rearrange("o (p c) -> (o p) c", c=PACK))
+        raw = {}
+
+        def load_piece(i, z):
+            raw[i, z] = arena.tile([P, PACK, P], F32, name=f"raw{i}{z}", offset=AT_RAW[i, z], align_bytes=64)
+            load_wb(raw[i, z], z, i * P, P)
+
+        load_piece(0, 0)
+        xw_all.append(arena.tile([P, T], I32, name="xw_all1", offset=AT_XW1, align_bytes=64))
+        nc.sync.dma_start(xw_all[1][:], xq_words[1].rearrange("p c r -> p (c r)").bitcast(I32))
+        wa_w = arena.tile([P, PASSES * 2 * N], U8, name="wa_w", offset=AT_WAW, align_bytes=64)
         nc.sync.dma_start(
             wa_w[:].bitcast(I32).rearrange("p (z c) -> p z c", z=PASSES),
             wa_words.bitcast(I32).rearrange("z p c -> p z c"),
         )
-        nc.sync.dma_start(xw_all[0][:], xq_words[0].rearrange("p c r -> p (c r)").bitcast(I32))
-        nc.sync.dma_start(xw_all[1][:], xq_words[1].rearrange("p c r -> p (c r)").bitcast(I32))
-
-        wa_s = keep.tile([P, PASSES * N], U8, name="wa_s", align_bytes=64)
-        nc.vector.memset(wa_s[:].bitcast(I32), 0)
-        for qd in range(QUADS):
-            nc.scalar.dma_start(
-                wa_s[:].bitcast(I32)[32 * qd : 32 * qd + 4, :].rearrange("p (z c) -> p z c", z=PASSES),
-                wa_scales.bitcast(I32)[:, 4 * qd : 4 * qd + 4, :].rearrange("z r c -> r z c"),
-            )
+        load_piece(0, 1)
+        wa_s = arena.tile([P, PASSES * N], U8, name="wa_s", offset=AT_WAS, align_bytes=64)
+        nc.gpsimd.memset(wa_s[:].bitcast(I32), 0)
+        load_scale_rows(nc.scalar, wa_s, wa_scales)
+        for i, z in PIECES[PASSES:]:
+            load_piece(i, z)
 
         ga_ps = psum.tile([P, PACK, P], F32, name="ga_ps")
         for c in range(PACK):
@@ -84,86 +108,146 @@ def tile_list_experts_disagreement_kernel(tc, xq_words, xq_scales, wa_words, wa_
         xw = [keep.tile([P, J], U32, name=f"xw{z}", align_bytes=64) for z in range(PASSES)]
         for z in range(PASSES):
             nc.vector.tensor_copy(xs[z][:], xs_all[:, z * T : (z + 1) * T].indirect(offsets[:]))
-        for z in range(PASSES):
+
+        def gather_words(z):
             nc.vector.tensor_copy(xw[z][:], xw_all[z][:].bitcast(U32).indirect(offsets[:]))
 
-        piece = PACK * P
-        raw = {}
-        for i in range(TILES):
-            for z in range(PASSES):
-                raw[i, z] = stage.tile([P, PACK, P], F32, name=f"raw{i}{z}", offset=(i * PASSES + z) * piece * 4)
-                nc.sync.dma_start(
-                    raw[i, z][:],
-                    wb[z * 512 : (z + 1) * 512, i * P : (i + 1) * P].rearrange("(p t) n -> p t n", t=PACK),
-                )
+        def round_rows(rows, grouped):
+            nc.scalar.copy(
+                grouped[:, :].rearrange("p (c i t) -> p c t i", i=4, t=PACK),
+                rows[:].rearrange("p t (c i) -> p c t i", i=4),
+            )
 
         p_ps = [psum.tile([P, J], F32, name=f"p_ps{i}", tag=f"bank{i}") for i in range(TILES)]
-        for z in range(PASSES):
-            for i in range(TILES):
-                nc.tensor.matmul_mx(
-                    out=p_ps[i][:],
-                    lhsT=wa_w[:, z * 2 * N + i * 2 * P : z * 2 * N + (i + 1) * 2 * P].bitcast(FP4X4),
-                    lhsT_scale=wa_s[:, z * N + i * P : z * N + (i + 1) * P],
-                    rhs=xw[z][:].bitcast(FP8X4),
-                    rhs_scale=xs[z][:],
-                    start=(z == 0),
-                    stop=(z == PASSES - 1),
-                )
 
-        def second_expert(i):
-            q_ps = psum.tile([P, J], F32, name=f"q_ps{i}", tag=("bank0" if i == TILES - 1 else f"qbank{i}"))
-            for z in range(PASSES):
-                grouped = keep.tile([P, piece], BF16, name=f"grouped{i}{z}", tag=f"grouped{i}{z}", align_bytes=64)
-                nc.scalar.copy(
-                    grouped[:].rearrange("p (c i t) -> p c t i", i=4, t=PACK),
-                    raw[i, z][:].rearrange("p t (c i) -> p c t i", i=4),
-                )
-                wb_w = keep.tile([P, P], U32, name=f"wb_w{i}{z}", align_bytes=64)
-                wb_s = keep.tile([P, P], U8, name=f"wb_s{i}{z}", align_bytes=64)
-                nc.vector.quantize_mx(out=wb_w[:].bitcast(FP8X4), scales=wb_s[:], in_=grouped[:])
-                nc.tensor.matmul_mx(
-                    out=q_ps[:],
-                    lhsT=wb_w[:].bitcast(FP8X4),
-                    lhsT_scale=wb_s[:],
-                    rhs=xw[z][:].bitcast(FP8X4),
-                    rhs_scale=xs[z][:],
-                    start=(z == 0),
-                    stop=(z == PASSES - 1),
-                )
-            return q_ps
+        def first_expert_pass(bank, i, z, start, stop):
+            nc.tensor.matmul_mx(
+                out=bank[:],
+                lhsT=wa_w[:, z * 2 * N + i * 2 * P : z * 2 * N + (i + 1) * 2 * P].bitcast(FP4X4),
+                lhsT_scale=wa_s[:, z * N + i * P : z * N + (i + 1) * P],
+                rhs=xw[z][:].bitcast(FP8X4),
+                rhs_scale=xs[z][:],
+                start=start,
+                stop=stop,
+            )
 
-        p_sb = keep.tile([P, J], F32, name="p_sb0")
-        nc.vector.tensor_copy(p_sb[:], p_ps[0][:])
-        q_ps = second_expert(0)
-        p_next = keep.tile([P, J], F32, name="p_sb1", tag="grouped01", align_bytes=64)
-        nc.vector.tensor_copy(p_next[:], p_ps[1][:])
+        def second_expert_pass(bank, words, plane, z, start, stop):
+            nc.tensor.matmul_mx(
+                out=bank[:],
+                lhsT=words.bitcast(FP8X4),
+                lhsT_scale=plane,
+                rhs=xw[z][:].bitcast(FP8X4),
+                rhs_scale=xs[z][:],
+                start=start,
+                stop=stop,
+            )
 
-        for i in range(TILES):
-            low = keep.tile([P, J], F32, name=f"low{i}")
-            nc.vector.tensor_tensor(low[:], q_ps[:], p_sb[:], ALU.min)
-            if i + 1 < TILES:
-                q_next = second_expert(i + 1)
-            if 1 <= i < TILES - 1:
-                p_next = keep.tile([P, J], F32, name=f"p_sb{i + 1}", tag=f"grouped{i}1", align_bytes=64)
-                nc.scalar.copy(p_next[:], p_ps[i + 1][:])
-            part = keep.tile([P, J], F32, name=f"part{i}")
-            nc.vector.scalar_tensor_tensor(part[:], low[:], 2.0, q_ps[:], ALU.mult, ALU.add)
-            whole = keep.tile([P, J], F32, name=f"whole{i}")
-            if i < 2:
-                nc.gpsimd.tensor_tensor(whole[:], part[:], p_sb[:], ALU.add)
+        def quantize(name, grouped, words):
+            plane = keep.tile([P, words.shape[1]], U8, name=f"plane{name}", align_bytes=64)
+            nc.vector.quantize_mx(out=words[:].bitcast(FP8X4), scales=plane[:], in_=grouped[:])
+            return plane
+
+        q_ps = [psum.tile([P, J], F32, name=f"q_ps{i}") for i in range(2)]
+
+        def early_piece(i, z):
+            if i == 0:
+                grouped = keep.tile([P, PACK * P], BF16, name=f"grouped{i}{z}", align_bytes=64)
             else:
-                nc.vector.tensor_tensor(whole[:], part[:], p_ps[i][:], ALU.add)
+                at = AT_XW1 + PIECES.index((i, z)) * KIB
+                grouped = arena.tile([P, PACK * P], BF16, name=f"grouped{i}{z}", offset=at, align_bytes=64)
+            round_rows(raw[i, z], grouped)
+            if (i, z) == (0, 1):
+                words = arena.tile([P, P], U32, name=f"words{i}{z}", offset=AT_XW1, align_bytes=64)
+            else:
+                words = keep.tile([P, P], U32, name=f"words{i}{z}", align_bytes=64)
+            plane = quantize(f"{i}{z}", grouped, words)
+            second_expert_pass(q_ps[i], words[:], plane[:], z, z == 0, z == PASSES - 1)
+
+        s_ps = {}
+
+        def late_tile(i):
+            first_expert_pass(p_ps[i], i, 1, True, False)
+            first_expert_pass(p_ps[i], i, 0, False, True)
+            s_ps[i] = psum.tile([P, J], F32, name=f"s_ps{i}", tag=("bank0" if i == TILES - 1 else "s_ps2"))
+            first_expert_pass(s_ps[i], i, 1, True, False)
+            first_expert_pass(s_ps[i], i, 0, False, False)
+            at = AT_XW1 + PIECES.index((i, 0)) * KIB
+            grouped = arena.tile([P, PASSES * PACK * P], BF16, name=f"grouped{i}", offset=at, align_bytes=64)
+            for z in range(PASSES):
+                round_rows(raw[i, z], grouped[:, z * PACK * P : (z + 1) * PACK * P])
+            words = arena.tile([P, PASSES * P], U32, name=f"words{i}", offset=AT_LOW[0] + (i - 2) * KIB, align_bytes=64)
+            plane = quantize(f"{i}", grouped, words)
+            for z in range(PASSES):
+                cols = slice(z * P, (z + 1) * P)
+                second_expert_pass(s_ps[i], words[:, cols], plane[:, cols], z, False, z == PASSES - 1)
+
+        low, part, whole = {}, {}, {}
+
+        def lower(i):
+            low[i] = arena.tile([P, J], F32, name=f"low{i}", offset=AT_LOW[i], align_bytes=64)
+            nc.vector.tensor_tensor(low[i][:], q_ps[i][:], p_sb[i][:], ALU.min)
+
+        def add_second(i):
+            part[i] = keep.tile([P, J], F32, name=f"part{i}")
+            nc.vector.scalar_tensor_tensor(part[i][:], low[i][:], 2.0, q_ps[i][:], ALU.mult, ALU.add)
+
+        def weigh(i):
             y = keep.tile([P, J], F32, name=f"y{i}")
             if i < 3:
-                nc.gpsimd.tensor_tensor(y[:], whole[:], ga4[:], ALU.mult)
+                nc.gpsimd.tensor_tensor(y[:], whole[i][:], ga4[:], ALU.mult)
             else:
                 nc.vector.scalar_tensor_tensor(
                     y[:].rearrange("p (n c) -> p n c", c=PACK),
-                    whole[:].rearrange("p (n c) -> p n c", c=PACK),
+                    whole[i][:].rearrange("p (n c) -> p n c", c=PACK),
                     0.25,
                     ga_by_j,
                     ALU.mult,
                     ALU.mult,
                 )
             nc.sync.dma_start(out[i * P : (i + 1) * P, :], y[:])
-            p_sb, q_ps = p_next, q_next
+
+        p_sb = {}
+        gather_words(0)
+        early_piece(0, 0)
+        first_expert_pass(p_ps[0], 0, 0, True, False)
+        gather_words(1)
+        first_expert_pass(p_ps[0], 0, 1, False, True)
+        early_piece(0, 1)
+        p_sb[0] = keep.tile([P, J], F32, name="p_sb0")
+        nc.vector.tensor_copy(p_sb[0][:], p_ps[0][:])
+        first_expert_pass(p_ps[1], 1, 1, True, False)
+        first_expert_pass(p_ps[1], 1, 0, False, True)
+        early_piece(1, 0)
+        lower(0)
+        early_piece(1, 1)
+        add_second(0)
+        late_tile(2)
+        p_sb[1] = arena.tile([P, J], F32, name="p_sb1", offset=AT_RAW[2, 1], align_bytes=64)
+        nc.scalar.copy(p_sb[1][:], p_ps[1][:])
+        lower(1)
+        late_tile(3)
+        whole[0] = arena.tile([P, J], F32, name="whole0", offset=AT_XW1 + 6 * KIB, align_bytes=64)
+        nc.gpsimd.tensor_tensor(whole[0][:], part[0][:], p_sb[0][:], ALU.add)
+        weigh(0)
+        add_second(1)
+        twice_p = arena.tile([P, 2 * J], F32, name="twice_p", offset=AT_RAW[3, 0], align_bytes=64)
+        for i in (2, 3):
+            nc.scalar.activation(twice_p[:, (i - 2) * J : (i - 1) * J], p_ps[i][:], ACT.Copy, scale=2.0)
+        apart, size = {}, {}
+
+        def difference(i):
+            apart[i] = keep.tile([P, J], F32, name=f"apart{i}")
+            nc.vector.tensor_tensor(apart[i][:], s_ps[i][:], twice_p[:, (i - 2) * J : (i - 1) * J], ALU.subtract)
+            size[i] = keep.tile([P, J], F32, name=f"size{i}")
+            nc.scalar.activation(size[i][:], apart[i][:], ACT.Abs)
+
+        difference(2)
+        whole[1] = keep.tile([P, J], F32, name="whole1")
+        nc.vector.tensor_tensor(whole[1][:], part[1][:], p_ps[1][:], ALU.add)
+        weigh(1)
+        difference(3)
+        for i in (2, 3):
+            whole[i] = keep.tile([P, J], F32, name=f"whole{i}")
+            nc.vector.scalar_tensor_tensor(whole[i][:], s_ps[i][:], 2.0, size[i][:], ALU.mult, ALU.subtract)
+        weigh(2)
+        weigh(3)

@@ -101,8 +101,6 @@ def tile_list_experts_disagreement_kernel(tc, xq_words, xq_scales, wa_words, wa_
         for c in range(PACK):
             nc.tensor.transpose(ga_ps[:, c, :], ga_rows[:, c : c + 1].to_broadcast([P, P]), ident[:])
         ga_by_j = ga_ps[:].rearrange("p c n -> p n c")
-        ga4 = keep.tile([P, J], F32, name="ga4")
-        nc.scalar.activation(ga4[:].rearrange("p (n c) -> p n c", c=PACK), ga_by_j, ACT.Copy, scale=0.25)
 
         xs = [keep.tile([P, J], U8, name=f"xs{z}", align_bytes=64) for z in range(PASSES)]
         xw = [keep.tile([P, J], U32, name=f"xw{z}", align_bytes=64) for z in range(PASSES)]
@@ -185,7 +183,7 @@ def tile_list_experts_disagreement_kernel(tc, xq_words, xq_scales, wa_words, wa_
 
         def lower(i):
             low[i] = arena.tile([P, J], F32, name=f"low{i}", offset=AT_LOW[i], align_bytes=64)
-            nc.vector.tensor_tensor(low[i][:], q_ps[i][:], p_sb[i][:], ALU.min)
+            nc.vector.tensor_tensor(low[i][:], q_ps[i][:], p_sb[i][:, :], ALU.min)
 
         def add_second(i):
             part[i] = keep.tile([P, J], F32, name=f"part{i}")
@@ -209,6 +207,8 @@ def tile_list_experts_disagreement_kernel(tc, xq_words, xq_scales, wa_words, wa_
         p_sb = {}
         gather_words(0)
         early_piece(0, 0)
+        ga4 = keep.tile([P, J], F32, name="ga4")
+        nc.scalar.activation(ga4[:].rearrange("p (n c) -> p n c", c=PACK), ga_by_j, ACT.Copy, scale=0.25)
         first_expert_pass(p_ps[0], 0, 0, True, False)
         gather_words(1)
         first_expert_pass(p_ps[0], 0, 1, False, True)
@@ -222,32 +222,35 @@ def tile_list_experts_disagreement_kernel(tc, xq_words, xq_scales, wa_words, wa_
         early_piece(1, 1)
         add_second(0)
         late_tile(2)
-        p_sb[1] = arena.tile([P, J], F32, name="p_sb1", offset=AT_RAW[2, 1], align_bytes=64)
-        nc.scalar.copy(p_sb[1][:], p_ps[1][:])
-        lower(1)
         late_tile(3)
         whole[0] = arena.tile([P, J], F32, name="whole0", offset=AT_XW1 + 6 * KIB, align_bytes=64)
         nc.gpsimd.tensor_tensor(whole[0][:], part[0][:], p_sb[0][:], ALU.add)
         weigh(0)
-        add_second(1)
-        twice_p = arena.tile([P, 2 * J], F32, name="twice_p", offset=AT_RAW[3, 0], align_bytes=64)
+        p_late = arena.tile([P, 3 * J], F32, name="p_late", offset=AT_RAW[2, 1], align_bytes=64)
+        p_sb[1] = p_late[:, :J]
+        nc.scalar.copy(p_sb[1], p_ps[1][:])
         for i in (2, 3):
-            nc.scalar.activation(twice_p[:, (i - 2) * J : (i - 1) * J], p_ps[i][:], ACT.Copy, scale=2.0)
+            nc.scalar.activation(p_late[:, (i - 1) * J : i * J], p_ps[i][:], ACT.Copy, scale=2.0)
         apart, size = {}, {}
 
         def difference(i):
             apart[i] = keep.tile([P, J], F32, name=f"apart{i}")
-            nc.vector.tensor_tensor(apart[i][:], s_ps[i][:], twice_p[:, (i - 2) * J : (i - 1) * J], ALU.subtract)
+            nc.vector.tensor_tensor(apart[i][:], s_ps[i][:], p_late[:, (i - 1) * J : i * J], ALU.subtract)
             size[i] = keep.tile([P, J], F32, name=f"size{i}")
             nc.scalar.activation(size[i][:], apart[i][:], ACT.Abs)
 
+        def less_difference(i):
+            whole[i] = keep.tile([P, J], F32, name=f"whole{i}")
+            nc.vector.scalar_tensor_tensor(whole[i][:], s_ps[i][:], 2.0, size[i][:], ALU.mult, ALU.subtract)
+
+        lower(1)
         difference(2)
+        add_second(1)
+        less_difference(2)
+        weigh(2)
+        difference(3)
         whole[1] = keep.tile([P, J], F32, name="whole1")
         nc.vector.tensor_tensor(whole[1][:], part[1][:], p_ps[1][:], ALU.add)
         weigh(1)
-        difference(3)
-        for i in (2, 3):
-            whole[i] = keep.tile([P, J], F32, name=f"whole{i}")
-            nc.vector.scalar_tensor_tensor(whole[i][:], s_ps[i][:], 2.0, size[i][:], ALU.mult, ALU.subtract)
-        weigh(2)
+        less_difference(3)
         weigh(3)

@@ -191,7 +191,7 @@ def tile_list_experts_disagreement_kernel(tc, xq_words, xq_scales, wa_words, wa_
 
         def weigh(i):
             y = keep.tile([P, J], F32, name=f"y{i}")
-            if i < 3:
+            if i < 2:
                 nc.gpsimd.tensor_tensor(y[:], whole[i][:], ga4[:], ALU.mult)
             else:
                 nc.vector.scalar_tensor_tensor(
@@ -246,11 +246,11 @@ def tile_list_experts_disagreement_kernel(tc, xq_words, xq_scales, wa_words, wa_
         lower(1)
         difference(2)
         add_second(1)
-        less_difference(2)
-        weigh(2)
         difference(3)
         whole[1] = keep.tile([P, J], F32, name="whole1")
         nc.vector.tensor_tensor(whole[1][:], part[1][:], p_ps[1][:], ALU.add)
         weigh(1)
+        less_difference(2)
         less_difference(3)
+        weigh(2)
         weigh(3)

from contextlib import ExitStack

import concourse.mybir as mybir

K, T, J, N = 1024, 2048, 512, 512
FLOPS = 2 * 2 * K * N * J

F32 = mybir.dt.float32
BF16 = mybir.dt.bfloat16
I32 = mybir.dt.int32
U32 = mybir.dt.uint32
U16 = mybir.dt.uint16
U8 = mybir.dt.uint8
FP8X4 = mybir.dt.float8_e4m3fn_x4
FP4X4 = mybir.dt.float4_e2m1fn_x4
ALU = mybir.AluOpType
ACT = mybir.ActivationFunctionType

P = 128
PACK = 4
K_PASS = P * PACK
PASSES = K // K_PASS
TILES = N // P
QUADS = 4
KIB = 1024

PIECES = [(i, z) for i in range(TILES) for z in range(PASSES)]
AT_XW1 = 0
AT_WAW = 8 * KIB
AT_WAS = 10 * KIB
AT_RAW = {piece: 11 * KIB + 2 * KIB * n for n, piece in enumerate(PIECES)}
AT_GA = AT_RAW[1, 0]
HELD_BYTES = 27 * KIB
AT_LOW = [HELD_BYTES + 2 * KIB * i for i in range(TILES)]


def tile_list_experts_disagreement_kernel(tc, xq_words, xq_scales, wa_words, wa_scales, wb, ga, offs, out):
    nc = tc.nc
    with ExitStack() as ctx:
        keep = ctx.enter_context(tc.tile_pool(name="keep", bufs=1))
        arena = ctx.enter_context(tc.tile_pool(name="arena", bufs=1))
        psum = ctx.enter_context(tc.psum_pool(name="psum", bufs=1))

        def load_scale_rows(queue, plane, scales):
            for qd in range(QUADS):
                queue.dma_start(
                    plane[:].bitcast(I32)[32 * qd : 32 * qd + 4, :].rearrange("p (z c) -> p z c", z=PASSES),
                    scales.bitcast(I32)[:, 4 * qd : 4 * qd + 4, :].rearrange("z r c -> r z c"),
                )

        def load_wb(raw, z, n0, width):
            rows = wb[z * K_PASS : (z + 1) * K_PASS, n0 : n0 + width]
            nc.sync.dma_start(raw[:], rows.rearrange("(p t) n -> p t n", t=PACK))

        offsets = keep.tile([P, J // 16], U16, name="offsets")
        nc.sync.dma_start(offsets[:], offs)
        xw_all = [keep.tile([P, T], I32, name="xw_all0", align_bytes=64)]
        nc.sync.dma_start(xw_all[0][:], xq_words[0].rearrange("p c r -> p (c r)").bitcast(I32))

        xs_all = keep.tile([P, PASSES * T], U8, name="xs_all", align_bytes=64)
        nc.vector.memset(xs_all[:].bitcast(I32), 0)
        load_scale_rows(nc.scalar, xs_all, xq_scales)

        blank = arena.tile([P, HELD_BYTES // 4], F32, name="blank", offset=0, align_bytes=64)
        nc.vector.memset(blank[:, :P], 0.0)
        ident = keep.tile([P, P], F32, name="ident")
        nc.gpsimd.affine_select(
            out=ident[:],
            in_=blank[:, :P],
            compare_op=ALU.not_equal,
            fill=1.0,
            base=0,
            pattern=[[-1, P]],
            channel_multiplier=1,
        )

        ga_rows = arena.tile([P, (HELD_BYTES - AT_GA) // 4], F32, name="ga_rows", offset=AT_GA, align_bytes=64)
        nc.sync.dma_start(ga_rows[:, :PACK], ga.rearrange("o (p c) -> (o p) c", c=PACK))
        raw = {}

        def load_piece(i, z):
            raw[i, z] = arena.tile([P, PACK, P], F32, name=f"raw{i}{z}", offset=AT_RAW[i, z], align_bytes=64)
            load_wb(raw[i, z], z, i * P, P)

        load_piece(0, 0)
        xw_all.append(arena.tile([P, T], I32, name="xw_all1", offset=AT_XW1, align_bytes=64))
        nc.sync.dma_start(xw_all[1][:], xq_words[1].rearrange("p c r -> p (c r)").bitcast(I32))
        wa_w = arena.tile([P, PASSES * 2 * N], U8, name="wa_w", offset=AT_WAW, align_bytes=64)
        nc.sync.dma_start(
            wa_w[:].bitcast(I32).rearrange("p (z c) -> p z c", z=PASSES),
            wa_words.bitcast(I32).rearrange("z p c -> p z c"),
        )
        load_piece(0, 1)
        wa_s = arena.tile([P, PASSES * N], U8, name="wa_s", offset=AT_WAS, align_bytes=64)
        nc.gpsimd.memset(wa_s[:].bitcast(I32), 0)
        load_scale_rows(nc.scalar, wa_s, wa_scales)
        for i, z in PIECES[PASSES:]:
            load_piece(i, z)

        ga_ps = psum.tile([P, PACK, P], F32, name="ga_ps")
        for c in range(PACK):
            nc.tensor.transpose(ga_ps[:, c, :], ga_rows[:, c : c + 1].to_broadcast([P, P]), ident[:])
        ga_by_j = ga_ps[:].rearrange("p c n -> p n c")

        xs = [keep.tile([P, J], U8, name=f"xs{z}", align_bytes=64) for z in range(PASSES)]
        xw = [keep.tile([P, J], U32, name=f"xw{z}", align_bytes=64) for z in range(PASSES)]
        for z in range(PASSES):
            nc.vector.tensor_copy(xs[z][:], xs_all[:, z * T : (z + 1) * T].indirect(offsets[:]))

        def gather_words(z):
            nc.vector.tensor_copy(xw[z][:], xw_all[z][:].bitcast(U32).indirect(offsets[:]))

        def round_rows(rows, grouped):
            nc.scalar.copy(
                grouped[:, :].rearrange("p (c i t) -> p c t i", i=4, t=PACK),
                rows[:].rearrange("p t (c i) -> p c t i", i=4),
            )

        p_ps = [psum.tile([P, J], F32, name=f"p_ps{i}", tag=f"bank{i}") for i in range(TILES)]

        def first_expert_pass(bank, i, z, start, stop):
            nc.tensor.matmul_mx(
                out=bank[:],
                lhsT=wa_w[:, z * 2 * N + i * 2 * P : z * 2 * N + (i + 1) * 2 * P].bitcast(FP4X4),
                lhsT_scale=wa_s[:, z * N + i * P : z * N + (i + 1) * P],
                rhs=xw[z][:].bitcast(FP8X4),
                rhs_scale=xs[z][:],
                start=start,
                stop=stop,
            )

        def second_expert_pass(bank, words, plane, z, start, stop):
            nc.tensor.matmul_mx(
                out=bank[:],
                lhsT=words.bitcast(FP8X4),
                lhsT_scale=plane,
                rhs=xw[z][:].bitcast(FP8X4),
                rhs_scale=xs[z][:],
                start=start,
                stop=stop,
            )

        def quantize(name, grouped, words):
            plane = keep.tile([P, words.shape[1]], U8, name=f"plane{name}", align_bytes=64)
            nc.vector.quantize_mx(out=words[:].bitcast(FP8X4), scales=plane[:], in_=grouped[:])
            return plane

        q_ps = [psum.tile([P, J], F32, name=f"q_ps{i}") for i in range(2)]

        def early_piece(i, z):
            if i == 0:
                grouped = keep.tile([P, PACK * P], BF16, name=f"grouped{i}{z}", align_bytes=64)
            else:
                at = AT_XW1 + PIECES.index((i, z)) * KIB
                grouped = arena.tile([P, PACK * P], BF16, name=f"grouped{i}{z}", offset=at, align_bytes=64)
            round_rows(raw[i, z], grouped)
            if (i, z) == (0, 1):
                words = arena.tile([P, P], U32, name=f"words{i}{z}", offset=AT_XW1, align_bytes=64)
            else:
                words = keep.tile([P, P], U32, name=f"words{i}{z}", align_bytes=64)
            plane = quantize(f"{i}{z}", grouped, words)
            second_expert_pass(q_ps[i], words[:], plane[:], z, z == 0, z == PASSES - 1)

        s_ps = {}

        def late_tile(i):
            first_expert_pass(p_ps[i], i, 1, True, False)
            first_expert_pass(p_ps[i], i, 0, False, True)
            s_ps[i] = psum.tile([P, J], F32, name=f"s_ps{i}", tag=("bank0" if i == TILES - 1 else "s_ps2"))
            first_expert_pass(s_ps[i], i, 1, True, False)
            first_expert_pass(s_ps[i], i, 0, False, False)
            at = AT_XW1 + PIECES.index((i, 0)) * KIB
            grouped = arena.tile([P, PASSES * PACK * P], BF16, name=f"grouped{i}", offset=at, align_bytes=64)
            for z in range(PASSES):
                round_rows(raw[i, z], grouped[:, z * PACK * P : (z + 1) * PACK * P])
            words = arena.tile([P, PASSES * P], U32, name=f"words{i}", offset=AT_LOW[0] + (i - 2) * KIB, align_bytes=64)
            plane = quantize(f"{i}", grouped, words)
            for z in range(PASSES):
                cols = slice(z * P, (z + 1) * P)
                second_expert_pass(s_ps[i], words[:, cols], plane[:, cols], z, False, z == PASSES - 1)

        low, part, whole = {}, {}, {}

        def lower(i):
            low[i] = arena.tile([P, J], F32, name=f"low{i}", offset=AT_LOW[i], align_bytes=64)
            nc.vector.tensor_tensor(low[i][:], q_ps[i][:], p_sb[i][:, :], ALU.min)

        def add_second(i):
            part[i] = keep.tile([P, J], F32, name=f"part{i}")
            nc.vector.scalar_tensor_tensor(part[i][:], low[i][:], 2.0, q_ps[i][:], ALU.mult, ALU.add)

        def weigh(i):
            y = keep.tile([P, J], F32, name=f"y{i}")
            if i < 2:
                nc.gpsimd.tensor_tensor(y[:], whole[i][:], ga4[:], ALU.mult)
            else:
                nc.vector.scalar_tensor_tensor(
                    y[:].rearrange("p (n c) -> p n c", c=PACK),
                    whole[i][:].rearrange("p (n c) -> p n c", c=PACK),
                    0.25,
                    ga_by_j,
                    ALU.mult,
                    ALU.mult,
                )
            nc.sync.dma_start(out[i * P : (i + 1) * P, :], y[:])

        p_sb = {}
        gather_words(0)
        early_piece(0, 0)
        ga4 = keep.tile([P, J], F32, name="ga4")
        nc.scalar.activation(ga4[:].rearrange("p (n c) -> p n c", c=PACK), ga_by_j, ACT.Copy, scale=0.25)
        first_expert_pass(p_ps[0], 0, 0, True, False)
        gather_words(1)
        first_expert_pass(p_ps[0], 0, 1, False, True)
        early_piece(0, 1)
        p_sb[0] = keep.tile([P, J], F32, name="p_sb0")
        nc.vector.tensor_copy(p_sb[0][:], p_ps[0][:])
        first_expert_pass(p_ps[1], 1, 1, True, False)
        first_expert_pass(p_ps[1], 1, 0, False, True)
        early_piece(1, 0)
        lower(0)
        early_piece(1, 1)
        add_second(0)
        late_tile(2)
        late_tile(3)
        whole[0] = arena.tile([P, J], F32, name="whole0", offset=AT_XW1 + 6 * KIB, align_bytes=64)
        nc.gpsimd.tensor_tensor(whole[0][:], part[0][:], p_sb[0][:], ALU.add)
        weigh(0)
        p_late = arena.tile([P, 3 * J], F32, name="p_late", offset=AT_RAW[2, 1], align_bytes=64)
        p_sb[1] = p_late[:, :J]
        nc.scalar.copy(p_sb[1], p_ps[1][:])
        for i in (2, 3):
            nc.scalar.activation(p_late[:, (i - 1) * J : i * J], p_ps[i][:], ACT.Copy, scale=2.0)
        apart, size = {}, {}

        def difference(i):
            apart[i] = keep.tile([P, J], F32, name=f"apart{i}")
            nc.vector.tensor_tensor(apart[i][:], s_ps[i][:], p_late[:, (i - 1) * J : i * J], ALU.subtract)
            size[i] = keep.tile([P, J], F32, name=f"size{i}")
            nc.scalar.activation(size[i][:], apart[i][:], ACT.Abs)

        def less_difference(i):
            whole[i] = keep.tile([P, J], F32, name=f"whole{i}")
            nc.vector.scalar_tensor_tensor(whole[i][:], s_ps[i][:], 2.0, size[i][:], ALU.mult, ALU.subtract)

        lower(1)
        difference(2)
        add_second(1)
        difference(3)
        whole[1] = keep.tile([P, J], F32, name="whole1")
        nc.vector.tensor_tensor(whole[1][:], part[1][:], p_ps[1][:], ALU.add)
        weigh(1)
        less_difference(2)
        less_difference(3)
        weigh(2)
        weigh(3)
